import numpy as np
import ml_dtypes


def mxq(x, axis, fmt="e4m3"):
    dtype, down = {"e4m3": (ml_dtypes.float8_e4m3fn, 7), "e5m2": (ml_dtypes.float8_e5m2, 14)}[fmt]
    v = np.moveaxis(np.asarray(x, np.float32).astype(ml_dtypes.bfloat16).astype(np.float64), axis, -1)
    blocks = v.reshape(v.shape[:-1] + (-1, 32))
    amax = np.abs(blocks).max(-1, keepdims=True)
    byte = np.maximum(np.where(amax > 0, np.frexp(amax)[1] - 1 + 127, 0) - down, 1)
    scale = np.exp2(byte - 127.0)
    codes = (blocks / scale).astype(np.float32).astype(dtype).astype(np.float64)
    return np.moveaxis((codes * scale).reshape(v.shape), -1, axis)


WIDE = False


def mx_kscale(k):
    if not WIDE:
        return np.ones(k)
    levels = np.array([10, -10, 5, -5, 0])
    if k % 512:
        return np.exp2(np.random.permutation(np.resize(levels, k // 32))).repeat(32)
    a = np.empty((k // 512, 16))
    for p in range(k // 512):
        a[p, :8] = np.random.permutation(np.resize(levels, 8))
        for g in range(8):
            far = levels[np.abs(levels - a[p, g]) >= 10]
            a[p, g + 8] = far[np.random.randint(len(far))]
    return np.exp2(a.ravel()).repeat(32)


BF16 = ml_dtypes.bfloat16


def bf(x):
    return np.asarray(x, np.float32).astype(BF16)


def f64(x):
    return np.asarray(x).astype(np.float64)


E2M1 = np.array([0.0, 0.5, 1.0, 1.5, 2.0, 3.0, 4.0, 6.0, -0.0, -0.5, -1.0, -1.5, -2.0, -3.0, -4.0, -6.0])


def pack_weight(w, fmt):
    k, n = w.shape
    w = f64(bf(w)).reshape(k // 32, 32, n)
    amax = np.abs(w).max(1)
    if fmt == "e4m3":
        byte = np.frexp(amax)[1] - 1 + 127 - 7
    else:
        mant, ex = np.frexp(amax / 6.0)
        byte = np.where(mant > 0.5, ex, ex - 1) + 127
    byte = np.clip(np.where(amax > 0, byte, 1), 1, 254)
    scaled = (w * np.exp2(127.0 - byte)[:, None, :]).reshape(k, n).astype(np.float32)
    by_word = np.ascontiguousarray(scaled.reshape(k // 512, 128, 4, n).transpose(0, 1, 3, 2))
    if fmt == "e4m3":
        words = by_word.astype(ml_dtypes.float8_e4m3fn).view(np.uint8)
    else:
        c = by_word.astype(ml_dtypes.float4_e2m1fn).view(np.uint8) & 0xF
        words = c[..., 0::2] | (c[..., 1::2] << 4)
    return np.ascontiguousarray(words), np.ascontiguousarray(byte.astype(np.uint8).reshape(k // 512, 16, n))


def unpack_weight(words, scales, fmt):
    g, p, n, _ = words.shape
    if fmt == "e4m3":
        vals = np.ascontiguousarray(words).view(ml_dtypes.float8_e4m3fn).astype(np.float64)
    else:
        nib = np.empty((g, p, n, 4), np.uint8)
        nib[..., 0::2] = words & 0xF
        nib[..., 1::2] = words >> 4
        vals = E2M1[nib]
    vals = vals * np.repeat(np.exp2(scales.astype(np.float64) - 127.0), 8, axis=1)[..., None]
    return vals.transpose(0, 1, 3, 2).reshape(g * 512, n)
def pack4(w):
    words, scales = pack_weight(w, "e2m1")
    return words.reshape(words.shape[0], 128, -1), scales


def unpack4(words, scales):
    return unpack_weight(words.reshape(words.shape[0], 128, -1, 2), scales, "e2m1")


M, C, F, D = 1024, 1024, 2048, 1024


def setup_inputs():
    s, t = mx_kscale(C), mx_kscale(F)
    wb_words, wb_scales = pack4(np.random.standard_normal((F, D)) / np.sqrt(F) / t[:, None])
    return {"dlog": bf(np.random.standard_normal((M, C)) * s),
            "wa": bf(np.random.standard_normal((D, C)) / np.sqrt(C) / s),
            "pred": bf(0.7 * np.random.standard_normal((M, F))),
            "teach": bf(0.7 * np.random.standard_normal((M, F))),
            "cw": bf((1 + 0.1 * np.random.standard_normal(F)) * t),
            "wb_words": wb_words,
            "wb_scales": wb_scales,
            "emb": bf(np.tanh(0.5 * np.random.standard_normal((M, D))))}


def reference(dlog, wa, pred, teach, cw, wb_words, wb_scales, emb):
    ga = mxq(f64(dlog), 1, "e4m3")
    ha = mxq(f64(wa), 1, "e4m3").T
    err = (f64(pred) - f64(teach)) * f64(cw)
    gb = mxq(err, 1, "e4m3")
    hb = unpack4(wb_words, wb_scales)
    de = (ga @ ha) + (gb @ hb)
    e = f64(emb)
    return de * (1 - e * e)

@@ -1,0 +1,341 @@
+from contextlib import ExitStack
+
+import concourse.mybir as mybir
+from concourse.masks import make_identity
+
+M, C, F, D = 1024, 1024, 2048, 1024
+FLOPS = 2 * M * D * (C + F)
+
+F32 = mybir.dt.float32
+BF16 = mybir.dt.bfloat16
+I32 = mybir.dt.int32
+U32 = mybir.dt.uint32
+U8 = mybir.dt.uint8
+FP8X4 = mybir.dt.float8_e4m3fn_x4
+FP4X4 = mybir.dt.float4_e2m1fn_x4
+ALU = mybir.AluOpType
+ACT = mybir.ActivationFunctionType
+
+P = 128
+K_PASS = 512
+N_TILE = 512
+BANK = 512
+TILES = M // P
+ERR_PASSES = F // K_PASS
+LOG_PASSES = C // K_PASS
+HALF = F // 2
+POOL_COLS = 1536
+POOL_FROM = 3
+
+
+def tile_two_loss_embedding_gradient_s1_kernel(
+    tc, dlog, wa, pred, teach, cw, wb_words, wb_scales, emb, out
+):
+    nc = tc.nc
+    with ExitStack() as ctx:
+        keep = ctx.enter_context(tc.tile_pool(name="keep", bufs=1))
+        work = ctx.enter_context(tc.tile_pool(name="work", bufs=1))
+        psum = ctx.enter_context(tc.psum_pool(name="psum", bufs=1))
+        ctx.enter_context(tc.manual_schedule())
+
+        def one_tile(x, i):
+            return x.rearrange("(s p j) f -> s j p f", p=P, j=2)[i // 2, i % 2]
+
+        def tile_pair(x, s):
+            return x.rearrange("(s p j) f -> s p (j f)", p=P, j=2)[s]
+
+        def load(name, src, dtype):
+            t = keep.tile(list(src.shape), dtype, name=name, align_bytes=64)
+            nc.sync.dma_start(out=t[:], in_=src)
+            return t
+
+        ident = keep.tile([P, P], F32, name="ident")
+        make_identity(nc, ident[:])
+        wb_plane = keep.tile([P, ERR_PASSES * D], U8, name="wb_plane", align_bytes=64)
+        nc.vector.memset(wb_plane[:].bitcast(I32), 0)
+
+        pt, dl, em, wa_rows, wb = {}, {}, {}, {}, {}
+
+        def load_pt_halves(i):
+            for h in range(2):
+                cols = slice(h * HALF, (h + 1) * HALF)
+                pt[i, h] = [load("%s%d_%d" % (nm, i, h), one_tile(x, i)[:, cols], BF16)[:] for nm, x in (("pred", pred), ("teach", teach))]
+
+        def load_pt(i):
+            pt[i] = [load("%s%d" % (nm, i), one_tile(x, i), BF16)[:] for nm, x in (("pred", pred), ("teach", teach))]
+
+        def load_pt_pair(s):
+            both = [load("%sp%d" % (nm, s), tile_pair(x, s), BF16) for nm, x in (("pred", pred), ("teach", teach))]
+            for j in range(2):
+                pt[2 * s + j] = [t[:, j * F : (j + 1) * F] for t in both]
+
+        def load_dl(s):
+            dl[s] = load("dl%d" % s, tile_pair(dlog, s), BF16)
+
+        def load_em(s):
+            em[s] = load("em%d" % s, tile_pair(emb, s), BF16)
+
+        def load_wa(s):
+            wa_rows[s] = load("wa%d" % s, tile_pair(wa, s), BF16)
+
+        def load_wb(a):
+            t = keep.tile([P, 2 * 2 * D], U8, name="wb%d" % a, align_bytes=64)
+            nc.sync.dma_start(
+                out=t[:].bitcast(I32).rearrange("p (g w) -> p g w", g=2),
+                in_=wb_words[2 * a : 2 * a + 2].bitcast(I32).rearrange("g p w -> p g w"),
+            )
+            wb[a] = t
+
+        def load_wb_scales():
+            rows = wb_scales.bitcast(I32).rearrange("g (q r) w -> r q g w", r=4)
+            plane = wb_plane[:].bitcast(I32).rearrange("p (g w) -> p g w", g=ERR_PASSES)
+            for r in range(4):
+                nc.sync.dma_start(out=plane[r:P:32], in_=rows[r])
+
+        cw_cols = keep.tile([P, 4 * ERR_PASSES], BF16, name="cw_cols")
+        nc.sync.dma_start(
+            out=cw_cols[:].rearrange("p (g t) -> p g t", t=4),
+            in_=cw.rearrange("(g p t) -> p g t", p=P, t=4),
+        )
+        load_pt_halves(0)
+        load_wa(0)
+        load_wa(1)
+        load_pt(1)
+        load_wb_scales()
+        load_dl(0)
+        load_wa(2)
+        load_wa(3)
+        load_pt(2)
+        load_wb(0)
+        load_wb(1)
+        load_pt(3)
+        load_em(0)
+        for s in range(1, 4):
+            if s > 1:
+                load_pt_pair(s)
+            load_dl(s)
+            load_em(s)
+
+        neg_cw = keep.tile([P, 4 * ERR_PASSES], BF16, name="neg_cw")
+        nc.scalar.activation(out=neg_cw[:], in_=cw_cols[:], func=ACT.Copy, scale=-1.0)
+        cw_bank = []
+        for h in range(2):
+            bank = psum.tile([P, BANK], F32, name="cw_bank%d" % h)
+            for u in range(2):
+                for g in range(2):
+                    c = 2 * (2 * h + g) + u
+                    nc.tensor.transpose(
+                        bank[:, (2 * u + g) * P : (2 * u + g + 1) * P],
+                        neg_cw[:].bitcast(F32)[:, c : c + 1].to_broadcast([P, P]),
+                        ident[:],
+                    )
+            cw_bank.append(bank)
+
+        wa_grouped, wa_q, diff, err, err_grouped, dl_grouped, err_q, dl_q, e2, acc, res = (
+            {}, {}, {}, {}, {}, {}, {}, {}, {}, {}, {}
+        )
+
+        def turn_bank(sources):
+            bank = psum.tile([P, BANK], F32, name="turned", bufs=3)
+            for c, src in enumerate(sources):
+                nc.tensor.transpose(bank[:, c * P : (c + 1) * P], src, ident[:])
+            return bank
+
+        def every_second_word(words, row, g, u):
+            base = row * (C // 2) + g * (K_PASS // 2)
+            return words[:, base + u : base + K_PASS // 2 : 2]
+
+        def quantize(name, grouped, bufs, pool):
+            width = grouped.shape[1] // 4
+            codes = pool.tile([P, width], U32, name=name + "_codes", align_bytes=64, bufs=bufs)
+            scales = pool.tile([P, width], U8, name=name + "_scales", align_bytes=64, bufs=bufs)
+            nc.vector.quantize_mx(out=codes[:].bitcast(FP8X4), scales=scales[:], in_=grouped)
+            return codes, scales
+
+        def turn_wa(s):
+            words = wa_rows[s][:].bitcast(F32)
+            for g in range(LOG_PASSES):
+                if s % 2 == 0:
+                    wa_grouped[s // 2, g] = keep.tile([P, 4 * N_TILE], BF16, name="wa_grouped%d_%d" % (s // 2, g), align_bytes=64)
+                bank = turn_bank([every_second_word(words, j, g, u) for j in range(2) for u in range(2)])
+                dst = wa_grouped[s // 2, g][:].bitcast(F32)[:, (s % 2) * BANK : (s % 2 + 1) * BANK]
+                nc.scalar.copy(out=dst.rearrange("p (r c) -> p r c", c=4), in_=bank[:].rearrange("p (c r) -> p r c", c=4))
+
+        def quantize_wa(n):
+            for g in range(LOG_PASSES):
+                wa_q[n, g] = quantize("wa%d_%d" % (n, g), wa_grouped[n, g][:], 1, keep)
+
+        def new_diff(i):
+            diff[i] = work.tile([P, F], F32, name="diff%d" % i, tag="stage%d" % (i % 2), align_bytes=64)
+
+        def subtract(engine, i, lo, hi):
+            engine.tensor_tensor(out=diff[i][:, lo:hi], in0=pt[i][0][:, lo:hi], in1=pt[i][1][:, lo:hi], op=ALU.subtract)
+
+        def subtract_first():
+            new_diff(0)
+            for h in range(2):
+                nc.vector.tensor_tensor(out=diff[0][:, h * HALF : (h + 1) * HALF], in0=pt[0, h][0], in1=pt[0, h][1], op=ALU.subtract)
+
+        def subtract_pool(i):
+            new_diff(i)
+            subtract(nc.gpsimd, i, 0, POOL_COLS)
+
+        def subtract_vector(i):
+            if i < POOL_FROM:
+                new_diff(i)
+                subtract(nc.vector, i, 0, F)
+            else:
+                subtract(nc.vector, i, POOL_COLS, F)
+
+        def weigh(i):
+            for h in range(2):
+                t = work.tile([P, HALF], BF16, name="err", bufs=4, align_bytes=64)
+                nc.vector.tensor_tensor(
+                    out=t[:].rearrange("p (u q e) -> p u q e", u=2, e=2),
+                    in0=diff[i][:, h * HALF : (h + 1) * HALF].rearrange("p (q u e) -> p u q e", u=2, e=2),
+                    in1=cw_bank[h][:].bitcast(BF16).rearrange("p (u q e) -> p u q e", u=2, e=2),
+                    op=ALU.mult,
+                )
+                err[i, h] = t
+
+        def turn_err(i):
+            err_grouped[i] = work.tile([P, F], BF16, name="err_grouped%d" % i, tag="stage%d" % (i % 2), align_bytes=64)
+            for h in range(2):
+                words = err[i, h][:].bitcast(F32)
+                bank = turn_bank([words[:, (2 * u + g) * P : (2 * u + g + 1) * P] for g in range(2) for u in range(2)])
+                dst = err_grouped[i][:].bitcast(F32)[:, h * BANK : (h + 1) * BANK]
+                nc.scalar.copy(
+                    out=dst.rearrange("p (g r u) -> p g r u", g=2, u=2),
+                    in_=bank[:].rearrange("p (g u r) -> p g r u", g=2, u=2),
+                )
+
+        def turn_dl(i):
+            words = dl[i // 2][:].bitcast(F32)
+            bank = turn_bank([every_second_word(words, i % 2, g, u) for g in range(LOG_PASSES) for u in range(2)])
+            t = work.tile([P, C], BF16, name="dl_grouped", bufs=3, align_bytes=64)
+            for g in range(LOG_PASSES):
+                cols = slice(g * K_PASS, (g + 1) * K_PASS)
+                nc.scalar.activation(
+                    out=t[:, cols].rearrange("p (r u e) -> p r u e", u=2, e=2),
+                    in_=bank[:].bitcast(BF16)[:, cols].rearrange("p (u r e) -> p r u e", u=2, e=2),
+                    func=ACT.Copy,
+                    scale=-1.0,
+                )
+            dl_grouped[i] = t
+
+        def quantize_dl(i):
+            dl_q[i] = quantize("dl", dl_grouped[i][:], 3, work)
+
+        def quantize_err(i):
+            codes, scales = quantize("err", err_grouped[i][:], 3, work)
+            for g in range(ERR_PASSES):
+                err_q[i, g] = (codes[:, g * P : (g + 1) * P], scales[:, g * P : (g + 1) * P])
+
+        def quantize_err_half(i, h):
+            codes, scales = quantize("err_half", err_grouped[i][:, h * HALF : (h + 1) * HALF], 2, work)
+            for g in range(2):
+                err_q[i, 2 * h + g] = (codes[:, g * P : (g + 1) * P], scales[:, g * P : (g + 1) * P])
+
+        def square(i):
+            t = work.tile([P, D], F32, name="e2", bufs=3)
+            nc.scalar.activation(out=t[:], in_=em[i // 2][:, (i % 2) * D : (i % 2 + 1) * D], func=ACT.Square)
+            e2[i] = t
+
+        def multiply_dl(i, n):
+            acc[i, n] = psum.tile([P, N_TILE], F32, name="acc", bufs=3)
+            codes, scales = dl_q[i]
+            for g in range(LOG_PASSES):
+                nc.tensor.matmul_mx(
+                    out=acc[i, n][:],
+                    lhsT=codes[:, g * P : (g + 1) * P].bitcast(FP8X4),
+                    lhsT_scale=scales[:, g * P : (g + 1) * P],
+                    rhs=wa_q[n, g][0][:].bitcast(FP8X4),
+                    rhs_scale=wa_q[n, g][1][:],
+                    start=(g == 0),
+                    stop=False,
+                )
+
+        def multiply_err(i, n, passes=range(ERR_PASSES)):
+            for g in passes:
+                byte0 = (g % 2) * 2 * D + n * 2 * N_TILE
+                col0 = g * D + n * N_TILE
+                nc.tensor.matmul_mx(
+                    out=acc[i, n][:],
+                    lhsT=err_q[i, g][0].bitcast(FP8X4),
+                    lhsT_scale=err_q[i, g][1],
+                    rhs=wb[g // 2][:, byte0 : byte0 + 2 * N_TILE].bitcast(FP4X4),
+                    rhs_scale=wb_plane[:, col0 : col0 + N_TILE],
+                    start=False,
+                    stop=(g == ERR_PASSES - 1),
+                )
+
+        def finish(i, n):
+            cols = slice(n * N_TILE, (n + 1) * N_TILE)
+            if n == 0:
+                res[i] = work.tile([P, D], F32, name="res", bufs=6)
+            nc.vector.scalar_tensor_tensor(
+                out=res[i][:, cols], in0=e2[i][:, cols], scalar=1.0, in1=acc[i, n][:], op0=ALU.subtract, op1=ALU.mult
+            )
+            if i == TILES - 1:
+                nc.sync.dma_start(out=one_tile(out, i)[:, cols], in_=res[i][:, cols])
+            elif n == 1:
+                nc.sync.dma_start(out=one_tile(out, i), in_=res[i][:])
+
+        subtract_first()
+        turn_wa(0)
+        turn_wa(1)
+        weigh(0)
+        turn_err(0)
+        quantize_wa(0)
+        subtract_vector(1)
+        quantize_err(0)
+        turn_dl(0)
+        quantize_dl(0)
+        turn_wa(2)
+        turn_wa(3)
+        turn_dl(1)
+        weigh(1)
+        multiply_dl(0, 0)
+        turn_err(1)
+        quantize_wa(1)
+        multiply_dl(0, 1)
+        quantize_dl(1)
+        subtract_vector(2)
+        quantize_err(1)
+        multiply_err(0, 0)
+        multiply_err(0, 1)
+        square(0)
+        square(1)
+        turn_dl(2)
+        for j in range(2, TILES):
+            if j + 1 < TILES:
+                subtract_pool(j + 1)
+            weigh(j)
+            if j == 2:
+                finish(0, 0)
+            finish(j - 2, 1)
+            multiply_dl(j - 1, 0)
+            multiply_err(j - 1, 0)
+            finish(j - 1, 0)
+            multiply_dl(j - 1, 1)
+            turn_err(j)
+            square(j)
+            multiply_err(j - 1, 1)
+            if j + 1 < TILES:
+                subtract_vector(j + 1)
+                turn_dl(j + 1)
+            quantize_dl(j)
+            if j + 1 < TILES:
+                quantize_err(j)
+        last = TILES - 1
+        quantize_err_half(last, 0)
+        quantize_err_half(last, 1)
+        finish(last - 1, 1)
+        multiply_dl(last, 0)
+        multiply_dl(last, 1)
+        multiply_err(last, 0, range(2))
+        multiply_err(last, 1, range(2))
+        multiply_err(last, 0, range(2, 4))
+        finish(last, 0)
+        multiply_err(last, 1, range(2, 4))
+        finish(last, 1)

@@ -24,8 +24,8 @@ TILES = M // P
 ERR_PASSES = F // K_PASS
 LOG_PASSES = C // K_PASS
 HALF = F // 2
-POOL_COLS = 1536
-POOL_FROM = 3
+POOL_COLS = 1408
+POOL_FROM = 4
 
 
 def tile_two_loss_embedding_gradient_s1_kernel(
@@ -56,8 +56,8 @@ def tile_two_loss_embedding_gradient_s1_kernel(
 
         pt, dl, em, wa_rows, wb = {}, {}, {}, {}, {}
 
-        def load_pt_halves(i):
-            for h in range(2):
+        def load_pt_half(i, h):
+            if True:
                 cols = slice(h * HALF, (h + 1) * HALF)
                 pt[i, h] = [load("%s%d_%d" % (nm, i, h), one_tile(x, i)[:, cols], BF16)[:] for nm, x in (("pred", pred), ("teach", teach))]
 
@@ -93,28 +93,35 @@ def tile_two_loss_embedding_gradient_s1_kernel(
                 nc.sync.dma_start(out=plane[r:P:32], in_=rows[r])
 
         cw_cols = keep.tile([P, 4 * ERR_PASSES], BF16, name="cw_cols")
-        nc.sync.dma_start(
-            out=cw_cols[:].rearrange("p (g t) -> p g t", t=4),
-            in_=cw.rearrange("(g p t) -> p g t", p=P, t=4),
-        )
-        load_pt_halves(0)
-        load_wa(0)
-        load_wa(1)
+
+        def load_cw():
+            nc.sync.dma_start(
+                out=cw_cols[:].rearrange("p (g t) -> p g t", t=4),
+                in_=cw.rearrange("(g p t) -> p g t", p=P, t=4),
+            )
+
+        load_pt_half(0, 0)
+        load_cw()
+        load_pt_half(0, 1)
         load_pt(1)
-        load_wb_scales()
+        for s in range(4):
+            load_wa(s)
         load_dl(0)
-        load_wa(2)
-        load_wa(3)
         load_pt(2)
+        load_wb_scales()
         load_wb(0)
         load_wb(1)
-        load_pt(3)
         load_em(0)
-        for s in range(1, 4):
-            if s > 1:
-                load_pt_pair(s)
-            load_dl(s)
-            load_em(s)
+        load_dl(1)
+        load_pt(3)
+        load_pt(4)
+        load_em(1)
+        load_dl(2)
+        load_pt(5)
+        load_em(2)
+        load_pt_pair(3)
+        load_dl(3)
+        load_em(3)
 
         neg_cw = keep.tile([P, 4 * ERR_PASSES], BF16, name="neg_cw")
         nc.scalar.activation(out=neg_cw[:], in_=cw_cols[:], func=ACT.Copy, scale=-1.0)
@@ -282,60 +289,76 @@ def tile_two_loss_embedding_gradient_s1_kernel(
                 nc.sync.dma_start(out=one_tile(out, i), in_=res[i][:])
 
         subtract_first()
-        turn_wa(0)
-        turn_wa(1)
         weigh(0)
         turn_err(0)
-        quantize_wa(0)
         subtract_vector(1)
         quantize_err(0)
+        weigh(1)
+        for s in range(4):
+            turn_wa(s)
+        quantize_wa(0)
+        quantize_wa(1)
         turn_dl(0)
         quantize_dl(0)
-        turn_wa(2)
-        turn_wa(3)
-        turn_dl(1)
-        weigh(1)
-        multiply_dl(0, 0)
         turn_err(1)
-        quantize_wa(1)
-        multiply_dl(0, 1)
-        quantize_dl(1)
+        turn_dl(1)
         subtract_vector(2)
+        quantize_dl(1)
         quantize_err(1)
+        multiply_dl(0, 0)
+        multiply_dl(0, 1)
         multiply_err(0, 0)
         multiply_err(0, 1)
         square(0)
+        weigh(2)
+        finish(0, 0)
+        finish(0, 1)
+        multiply_dl(1, 0)
+        multiply_err(1, 0)
         square(1)
+        finish(1, 0)
         turn_dl(2)
-        for j in range(2, TILES):
-            if j + 1 < TILES:
-                subtract_pool(j + 1)
+        turn_err(2)
+        multiply_dl(1, 1)
+        multiply_err(1, 1)
+        subtract_vector(3)
+        turn_dl(3)
+        square(2)
+        quantize_dl(2)
+        quantize_err(2)
+        last = TILES - 1
+        for j in range(3, last):
+            subtract_pool(j + 1)
             weigh(j)
-            if j == 2:
-                finish(0, 0)
             finish(j - 2, 1)
             multiply_dl(j - 1, 0)
             multiply_err(j - 1, 0)
             finish(j - 1, 0)
             multiply_dl(j - 1, 1)
             turn_err(j)
+            turn_dl(j + 1)
             square(j)
             multiply_err(j - 1, 1)
-            if j + 1 < TILES:
-                subtract_vector(j + 1)
-                turn_dl(j + 1)
+            subtract_vector(j + 1)
             quantize_dl(j)
-            if j + 1 < TILES:
-                quantize_err(j)
-        last = TILES - 1
+            quantize_err(j)
+        weigh(last)
+        finish(last - 2, 1)
+        multiply_dl(last - 1, 0)
+        multiply_err(last - 1, 0)
+        multiply_dl(last - 1, 1)
+        multiply_err(last - 1, 1, range(2))
+        turn_err(last)
+        square(last)
+        multiply_err(last - 1, 1, range(2, 4))
+        quantize_dl(last)
+        finish(last - 1, 0)
         quantize_err_half(last, 0)
         quantize_err_half(last, 1)
         finish(last - 1, 1)
         multiply_dl(last, 0)
         multiply_dl(last, 1)
-        multiply_err(last, 0, range(2))
-        multiply_err(last, 1, range(2))
-        multiply_err(last, 0, range(2, 4))
+        multiply_err(last, 0)
         finish(last, 0)
-        multiply_err(last, 1, range(2, 4))
+        multiply_err(last, 1)
         finish(last, 1)

@@ -24,8 +24,12 @@ TILES = M // P
 ERR_PASSES = F // K_PASS
 LOG_PASSES = C // K_PASS
 HALF = F // 2
-POOL_COLS = 1408
+POOL_COLS = 1472
 POOL_FROM = 4
+TURN_BANKS = 3
+ACC_BANKS = 3
+OPERAND_BUFS = 3
+RESULT_BUFS = 6
 
 
 def tile_two_loss_embedding_gradient_s1_kernel(
@@ -41,56 +45,55 @@ def tile_two_loss_embedding_gradient_s1_kernel(
         def one_tile(x, i):
             return x.rearrange("(s p j) f -> s j p f", p=P, j=2)[i // 2, i % 2]
 
-        def tile_pair(x, s):
+        def tile_couple(x, s):
             return x.rearrange("(s p j) f -> s p (j f)", p=P, j=2)[s]
 
-        def load(name, src, dtype):
-            t = keep.tile(list(src.shape), dtype, name=name, align_bytes=64)
+        def load(name, src):
+            t = keep.tile(list(src.shape), BF16, name=name, align_bytes=64)
             nc.sync.dma_start(out=t[:], in_=src)
             return t
 
         ident = keep.tile([P, P], F32, name="ident")
         make_identity(nc, ident[:])
-        wb_plane = keep.tile([P, ERR_PASSES * D], U8, name="wb_plane", align_bytes=64)
-        nc.vector.memset(wb_plane[:].bitcast(I32), 0)
+        wb_scale_rows = keep.tile([P, ERR_PASSES * D], U8, name="wb_scale_rows", align_bytes=64)
+        nc.vector.memset(wb_scale_rows[:].bitcast(I32), 0)
 
-        pt, dl, em, wa_rows, wb = {}, {}, {}, {}, {}
+        first_halves, pred_teach, dlog_rows, emb_rows, wa_rows, wb_codes = {}, {}, {}, {}, {}, {}
 
-        def load_pt_half(i, h):
-            if True:
-                cols = slice(h * HALF, (h + 1) * HALF)
-                pt[i, h] = [load("%s%d_%d" % (nm, i, h), one_tile(x, i)[:, cols], BF16)[:] for nm, x in (("pred", pred), ("teach", teach))]
+        def load_first_half(h):
+            cols = slice(h * HALF, (h + 1) * HALF)
+            first_halves[h] = (load("pred0_%d" % h, one_tile(pred, 0)[:, cols]), load("teach0_%d" % h, one_tile(teach, 0)[:, cols]))
 
-        def load_pt(i):
-            pt[i] = [load("%s%d" % (nm, i), one_tile(x, i), BF16)[:] for nm, x in (("pred", pred), ("teach", teach))]
+        def load_pred_teach(i):
+            pred_teach[i] = (load("pred%d" % i, one_tile(pred, i))[:], load("teach%d" % i, one_tile(teach, i))[:])
 
-        def load_pt_pair(s):
-            both = [load("%sp%d" % (nm, s), tile_pair(x, s), BF16) for nm, x in (("pred", pred), ("teach", teach))]
+        def load_dlog_couple(s):
+            t = load("dlog_couple%d" % s, tile_couple(dlog, s))
             for j in range(2):
-                pt[2 * s + j] = [t[:, j * F : (j + 1) * F] for t in both]
+                dlog_rows[2 * s + j] = (t, j)
 
-        def load_dl(s):
-            dl[s] = load("dl%d" % s, tile_pair(dlog, s), BF16)
+        def load_dlog_tile(i):
+            dlog_rows[i] = (load("dlog%d" % i, one_tile(dlog, i)), 0)
 
-        def load_em(s):
-            em[s] = load("em%d" % s, tile_pair(emb, s), BF16)
+        def load_emb(s):
+            emb_rows[s] = load("emb%d" % s, tile_couple(emb, s))
 
         def load_wa(s):
-            wa_rows[s] = load("wa%d" % s, tile_pair(wa, s), BF16)
+            wa_rows[s] = load("wa%d" % s, tile_couple(wa, s))
 
-        def load_wb(a):
-            t = keep.tile([P, 2 * 2 * D], U8, name="wb%d" % a, align_bytes=64)
+        def load_wb(h):
+            t = keep.tile([P, 2 * 2 * D], U8, name="wb%d" % h, align_bytes=64)
             nc.sync.dma_start(
                 out=t[:].bitcast(I32).rearrange("p (g w) -> p g w", g=2),
-                in_=wb_words[2 * a : 2 * a + 2].bitcast(I32).rearrange("g p w -> p g w"),
+                in_=wb_words[2 * h : 2 * h + 2].bitcast(I32).rearrange("g p w -> p g w"),
             )
-            wb[a] = t
+            wb_codes[h] = t
 
         def load_wb_scales():
             rows = wb_scales.bitcast(I32).rearrange("g (q r) w -> r q g w", r=4)
-            plane = wb_plane[:].bitcast(I32).rearrange("p (g w) -> p g w", g=ERR_PASSES)
+            dst = wb_scale_rows[:].bitcast(I32).rearrange("p (g w) -> p g w", g=ERR_PASSES)
             for r in range(4):
-                nc.sync.dma_start(out=plane[r:P:32], in_=rows[r])
+                nc.sync.dma_start(out=dst[r:P:32], in_=rows[r])
 
         cw_cols = keep.tile([P, 4 * ERR_PASSES], BF16, name="cw_cols")
 
@@ -100,28 +103,27 @@ def tile_two_loss_embedding_gradient_s1_kernel(
                 in_=cw.rearrange("(g p t) -> p g t", p=P, t=4),
             )
 
-        load_pt_half(0, 0)
+        load_first_half(0)
         load_cw()
-        load_pt_half(0, 1)
-        load_pt(1)
-        for s in range(4):
+        load_first_half(1)
+        load_pred_teach(1)
+        for s in range(D // (2 * P)):
             load_wa(s)
-        load_dl(0)
-        load_pt(2)
+        load_dlog_couple(0)
+        load_pred_teach(2)
         load_wb_scales()
         load_wb(0)
         load_wb(1)
-        load_em(0)
-        load_dl(1)
-        load_pt(3)
-        load_pt(4)
-        load_em(1)
-        load_dl(2)
-        load_pt(5)
-        load_em(2)
-        load_pt_pair(3)
-        load_dl(3)
-        load_em(3)
+        load_emb(0)
+        load_dlog_tile(2)
+        load_pred_teach(3)
+        load_dlog_tile(3)
+        for s in range(1, TILES // 2 - 1):
+            load_pred_teach(2 * s + 2)
+            load_emb(s)
+            load_dlog_couple(s + 1)
+            load_pred_teach(2 * s + 3)
+        load_emb(TILES // 2 - 1)
 
         neg_cw = keep.tile([P, 4 * ERR_PASSES], BF16, name="neg_cw")
         nc.scalar.activation(out=neg_cw[:], in_=cw_cols[:], func=ACT.Copy, scale=-1.0)
@@ -130,27 +132,26 @@ def tile_two_loss_embedding_gradient_s1_kernel(
             bank = psum.tile([P, BANK], F32, name="cw_bank%d" % h)
             for u in range(2):
                 for g in range(2):
-                    c = 2 * (2 * h + g) + u
+                    pair = 2 * (2 * h + g) + u
                     nc.tensor.transpose(
                         bank[:, (2 * u + g) * P : (2 * u + g + 1) * P],
-                        neg_cw[:].bitcast(F32)[:, c : c + 1].to_broadcast([P, P]),
+                        neg_cw[:].bitcast(F32)[:, pair : pair + 1].to_broadcast([P, P]),
                         ident[:],
                     )
             cw_bank.append(bank)
 
-        wa_grouped, wa_q, diff, err, err_grouped, dl_grouped, err_q, dl_q, e2, acc, res = (
-            {}, {}, {}, {}, {}, {}, {}, {}, {}, {}, {}
-        )
+        wa_grouped, wa_q, diff, err, err_grouped, err_q = {}, {}, {}, {}, {}, {}
+        dlog_grouped, dlog_q, emb_sq, acc, result = {}, {}, {}, {}, {}
 
         def turn_bank(sources):
-            bank = psum.tile([P, BANK], F32, name="turned", bufs=3)
+            bank = psum.tile([P, BANK], F32, name="turned", bufs=TURN_BANKS)
             for c, src in enumerate(sources):
                 nc.tensor.transpose(bank[:, c * P : (c + 1) * P], src, ident[:])
             return bank
 
-        def every_second_word(words, row, g, u):
-            base = row * (C // 2) + g * (K_PASS // 2)
-            return words[:, base + u : base + K_PASS // 2 : 2]
+        def pairs_of_pass(rows, j, g, u):
+            base = j * (C // 2) + g * (K_PASS // 2)
+            return rows[:].bitcast(F32)[:, base + u : base + K_PASS // 2 : 2]
 
         def quantize(name, grouped, bufs, pool):
             width = grouped.shape[1] // 4
@@ -160,13 +161,16 @@ def tile_two_loss_embedding_gradient_s1_kernel(
             return codes, scales
 
         def turn_wa(s):
-            words = wa_rows[s][:].bitcast(F32)
             for g in range(LOG_PASSES):
                 if s % 2 == 0:
-                    wa_grouped[s // 2, g] = keep.tile([P, 4 * N_TILE], BF16, name="wa_grouped%d_%d" % (s // 2, g), align_bytes=64)
-                bank = turn_bank([every_second_word(words, j, g, u) for j in range(2) for u in range(2)])
+                    wa_grouped[s // 2, g] = keep.tile(
+                        [P, 4 * N_TILE], BF16, name="wa_grouped%d_%d" % (s // 2, g), align_bytes=64
+                    )
+                bank = turn_bank([pairs_of_pass(wa_rows[s], j, g, u) for j in range(2) for u in range(2)])
                 dst = wa_grouped[s // 2, g][:].bitcast(F32)[:, (s % 2) * BANK : (s % 2 + 1) * BANK]
-                nc.scalar.copy(out=dst.rearrange("p (r c) -> p r c", c=4), in_=bank[:].rearrange("p (c r) -> p r c", c=4))
+                nc.scalar.copy(
+                    out=dst.rearrange("p (r ju) -> p r ju", ju=4), in_=bank[:].rearrange("p (ju r) -> p r ju", ju=4)
+                )
 
         def quantize_wa(n):
             for g in range(LOG_PASSES):
@@ -176,12 +180,16 @@ def tile_two_loss_embedding_gradient_s1_kernel(
             diff[i] = work.tile([P, F], F32, name="diff%d" % i, tag="stage%d" % (i % 2), align_bytes=64)
 
         def subtract(engine, i, lo, hi):
-            engine.tensor_tensor(out=diff[i][:, lo:hi], in0=pt[i][0][:, lo:hi], in1=pt[i][1][:, lo:hi], op=ALU.subtract)
+            pred_i, teach_i = pred_teach[i]
+            engine.tensor_tensor(out=diff[i][:, lo:hi], in0=pred_i[:, lo:hi], in1=teach_i[:, lo:hi], op=ALU.subtract)
 
         def subtract_first():
             new_diff(0)
             for h in range(2):
-                nc.vector.tensor_tensor(out=diff[0][:, h * HALF : (h + 1) * HALF], in0=pt[0, h][0], in1=pt[0, h][1], op=ALU.subtract)
+                pred_h, teach_h = first_halves[h]
+                nc.vector.tensor_tensor(
+                    out=diff[0][:, h * HALF : (h + 1) * HALF], in0=pred_h[:], in1=teach_h[:], op=ALU.subtract
+                )
 
         def subtract_pool(i):
             new_diff(i)
@@ -198,9 +206,9 @@ def tile_two_loss_embedding_gradient_s1_kernel(
             for h in range(2):
                 t = work.tile([P, HALF], BF16, name="err", bufs=4, align_bytes=64)
                 nc.vector.tensor_tensor(
-                    out=t[:].rearrange("p (u q e) -> p u q e", u=2, e=2),
-                    in0=diff[i][:, h * HALF : (h + 1) * HALF].rearrange("p (q u e) -> p u q e", u=2, e=2),
-                    in1=cw_bank[h][:].bitcast(BF16).rearrange("p (u q e) -> p u q e", u=2, e=2),
+                    out=t[:].rearrange("m (u q e) -> m u q e", u=2, e=2),
+                    in0=diff[i][:, h * HALF : (h + 1) * HALF].rearrange("m (q u e) -> m u q e", u=2, e=2),
+                    in1=cw_bank[h][:].bitcast(BF16).rearrange("m (u q e) -> m u q e", u=2, e=2),
                     op=ALU.mult,
                 )
                 err[i, h] = t
@@ -208,18 +216,18 @@ def tile_two_loss_embedding_gradient_s1_kernel(
         def turn_err(i):
             err_grouped[i] = work.tile([P, F], BF16, name="err_grouped%d" % i, tag="stage%d" % (i % 2), align_bytes=64)
             for h in range(2):
-                words = err[i, h][:].bitcast(F32)
-                bank = turn_bank([words[:, (2 * u + g) * P : (2 * u + g + 1) * P] for g in range(2) for u in range(2)])
+                pairs = err[i, h][:].bitcast(F32)
+                bank = turn_bank([pairs[:, (2 * u + g) * P : (2 * u + g + 1) * P] for g in range(2) for u in range(2)])
                 dst = err_grouped[i][:].bitcast(F32)[:, h * BANK : (h + 1) * BANK]
                 nc.scalar.copy(
                     out=dst.rearrange("p (g r u) -> p g r u", g=2, u=2),
                     in_=bank[:].rearrange("p (g u r) -> p g r u", g=2, u=2),
                 )
 
-        def turn_dl(i):
-            words = dl[i // 2][:].bitcast(F32)
-            bank = turn_bank([every_second_word(words, i % 2, g, u) for g in range(LOG_PASSES) for u in range(2)])
-            t = work.tile([P, C], BF16, name="dl_grouped", bufs=3, align_bytes=64)
+        def turn_dlog(i):
+            rows, j = dlog_rows[i]
+            bank = turn_bank([pairs_of_pass(rows, j, g, u) for g in range(LOG_PASSES) for u in range(2)])
+            t = work.tile([P, C], BF16, name="dlog_grouped", bufs=OPERAND_BUFS, align_bytes=64)
             for g in range(LOG_PASSES):
                 cols = slice(g * K_PASS, (g + 1) * K_PASS)
                 nc.scalar.activation(
@@ -228,13 +236,13 @@ def tile_two_loss_embedding_gradient_s1_kernel(
                     func=ACT.Copy,
                     scale=-1.0,
                 )
-            dl_grouped[i] = t
+            dlog_grouped[i] = t
 
-        def quantize_dl(i):
-            dl_q[i] = quantize("dl", dl_grouped[i][:], 3, work)
+        def quantize_dlog(i):
+            dlog_q[i] = quantize("dlog", dlog_grouped[i][:], OPERAND_BUFS, work)
 
         def quantize_err(i):
-            codes, scales = quantize("err", err_grouped[i][:], 3, work)
+            codes, scales = quantize("err", err_grouped[i][:], OPERAND_BUFS, work)
             for g in range(ERR_PASSES):
                 err_q[i, g] = (codes[:, g * P : (g + 1) * P], scales[:, g * P : (g + 1) * P])
 
@@ -244,13 +252,13 @@ def tile_two_loss_embedding_gradient_s1_kernel(
                 err_q[i, 2 * h + g] = (codes[:, g * P : (g + 1) * P], scales[:, g * P : (g + 1) * P])
 
         def square(i):
-            t = work.tile([P, D], F32, name="e2", bufs=3)
-            nc.scalar.activation(out=t[:], in_=em[i // 2][:, (i % 2) * D : (i % 2 + 1) * D], func=ACT.Square)
-            e2[i] = t
+            t = work.tile([P, D], F32, name="emb_sq", bufs=OPERAND_BUFS)
+            nc.scalar.activation(out=t[:], in_=emb_rows[i // 2][:, (i % 2) * D : (i % 2 + 1) * D], func=ACT.Square)
+            emb_sq[i] = t
 
-        def multiply_dl(i, n):
-            acc[i, n] = psum.tile([P, N_TILE], F32, name="acc", bufs=3)
-            codes, scales = dl_q[i]
+        def multiply_dlog(i, n):
+            acc[i, n] = psum.tile([P, N_TILE], F32, name="acc", bufs=ACC_BANKS)
+            codes, scales = dlog_q[i]
             for g in range(LOG_PASSES):
                 nc.tensor.matmul_mx(
                     out=acc[i, n][:],
@@ -270,8 +278,8 @@ def tile_two_loss_embedding_gradient_s1_kernel(
                     out=acc[i, n][:],
                     lhsT=err_q[i, g][0].bitcast(FP8X4),
                     lhsT_scale=err_q[i, g][1],
-                    rhs=wb[g // 2][:, byte0 : byte0 + 2 * N_TILE].bitcast(FP4X4),
-                    rhs_scale=wb_plane[:, col0 : col0 + N_TILE],
+                    rhs=wb_codes[g // 2][:, byte0 : byte0 + 2 * N_TILE].bitcast(FP4X4),
+                    rhs_scale=wb_scale_rows[:, col0 : col0 + N_TILE],
                     start=False,
                     stop=(g == ERR_PASSES - 1),
                 )
@@ -279,14 +287,19 @@ def tile_two_loss_embedding_gradient_s1_kernel(
         def finish(i, n):
             cols = slice(n * N_TILE, (n + 1) * N_TILE)
             if n == 0:
-                res[i] = work.tile([P, D], F32, name="res", bufs=6)
+                result[i] = work.tile([P, D], F32, name="result", bufs=RESULT_BUFS)
             nc.vector.scalar_tensor_tensor(
-                out=res[i][:, cols], in0=e2[i][:, cols], scalar=1.0, in1=acc[i, n][:], op0=ALU.subtract, op1=ALU.mult
+                out=result[i][:, cols],
+                in0=emb_sq[i][:, cols],
+                scalar=1.0,
+                in1=acc[i, n][:],
+                op0=ALU.subtract,
+                op1=ALU.mult,
             )
             if i == TILES - 1:
-                nc.sync.dma_start(out=one_tile(out, i)[:, cols], in_=res[i][:, cols])
+                nc.sync.dma_start(out=one_tile(out, i)[:, cols], in_=result[i][:, cols])
             elif n == 1:
-                nc.sync.dma_start(out=one_tile(out, i), in_=res[i][:])
+                nc.sync.dma_start(out=one_tile(out, i), in_=result[i][:])
 
         subtract_first()
         weigh(0)
@@ -294,70 +307,73 @@ def tile_two_loss_embedding_gradient_s1_kernel(
         subtract_vector(1)
         quantize_err(0)
         weigh(1)
-        for s in range(4):
+        for s in range(D // (2 * P)):
             turn_wa(s)
         quantize_wa(0)
         quantize_wa(1)
-        turn_dl(0)
-        quantize_dl(0)
+        turn_dlog(0)
+        quantize_dlog(0)
         turn_err(1)
-        turn_dl(1)
+        turn_dlog(1)
         subtract_vector(2)
-        quantize_dl(1)
+        quantize_dlog(1)
         quantize_err(1)
-        multiply_dl(0, 0)
-        multiply_dl(0, 1)
+
+        multiply_dlog(0, 0)
+        multiply_dlog(0, 1)
         multiply_err(0, 0)
         multiply_err(0, 1)
         square(0)
         weigh(2)
         finish(0, 0)
         finish(0, 1)
-        multiply_dl(1, 0)
+        multiply_dlog(1, 0)
         multiply_err(1, 0)
         square(1)
         finish(1, 0)
-        turn_dl(2)
+        turn_dlog(2)
         turn_err(2)
-        multiply_dl(1, 1)
+        multiply_dlog(1, 1)
         multiply_err(1, 1)
         subtract_vector(3)
-        turn_dl(3)
+        turn_dlog(3)
         square(2)
-        quantize_dl(2)
+        quantize_dlog(2)
         quantize_err(2)
+
         last = TILES - 1
-        for j in range(3, last):
-            subtract_pool(j + 1)
-            weigh(j)
-            finish(j - 2, 1)
-            multiply_dl(j - 1, 0)
-            multiply_err(j - 1, 0)
-            finish(j - 1, 0)
-            multiply_dl(j - 1, 1)
-            turn_err(j)
-            turn_dl(j + 1)
-            square(j)
-            multiply_err(j - 1, 1)
-            subtract_vector(j + 1)
-            quantize_dl(j)
-            quantize_err(j)
+        for i in range(POOL_FROM - 1, last):
+            subtract_pool(i + 1)
+            weigh(i)
+            finish(i - 2, 1)
+            multiply_dlog(i - 1, 0)
+            multiply_err(i - 1, 0)
+            finish(i - 1, 0)
+            multiply_dlog(i - 1, 1)
+            turn_err(i)
+            turn_dlog(i + 1)
+            square(i)
+            multiply_err(i - 1, 1)
+            subtract_vector(i + 1)
+            quantize_dlog(i)
+            quantize_err(i)
+
         weigh(last)
         finish(last - 2, 1)
-        multiply_dl(last - 1, 0)
+        multiply_dlog(last - 1, 0)
         multiply_err(last - 1, 0)
-        multiply_dl(last - 1, 1)
+        multiply_dlog(last - 1, 1)
         multiply_err(last - 1, 1, range(2))
         turn_err(last)
         square(last)
-        multiply_err(last - 1, 1, range(2, 4))
-        quantize_dl(last)
+        multiply_err(last - 1, 1, range(2, ERR_PASSES))
+        quantize_dlog(last)
         finish(last - 1, 0)
         quantize_err_half(last, 0)
         quantize_err_half(last, 1)
         finish(last - 1, 1)
-        multiply_dl(last, 0)
-        multiply_dl(last, 1)
+        multiply_dlog(last, 0)
+        multiply_dlog(last, 1)
         multiply_err(last, 0)
         finish(last, 0)
         multiply_err(last, 1)

from contextlib import ExitStack

import concourse.mybir as mybir
from concourse.masks import make_identity

M, C, F, D = 1024, 1024, 2048, 1024
FLOPS = 2 * M * D * (C + F)

F32 = mybir.dt.float32
BF16 = mybir.dt.bfloat16
I32 = mybir.dt.int32
U32 = mybir.dt.uint32
U8 = mybir.dt.uint8
FP8X4 = mybir.dt.float8_e4m3fn_x4
FP4X4 = mybir.dt.float4_e2m1fn_x4
ALU = mybir.AluOpType
ACT = mybir.ActivationFunctionType

P = 128
K_PASS = 512
N_TILE = 512
BANK = 512
TILES = M // P
ERR_PASSES = F // K_PASS
LOG_PASSES = C // K_PASS
HALF = F // 2
POOL_COLS = 1472
POOL_FROM = 4
TURN_BANKS = 3
ACC_BANKS = 3
OPERAND_BUFS = 3
RESULT_BUFS = 6


def tile_two_loss_embedding_gradient_s1_kernel(
    tc, dlog, wa, pred, teach, cw, wb_words, wb_scales, emb, out
):
    nc = tc.nc
    with ExitStack() as ctx:
        keep = ctx.enter_context(tc.tile_pool(name="keep", bufs=1))
        work = ctx.enter_context(tc.tile_pool(name="work", bufs=1))
        psum = ctx.enter_context(tc.psum_pool(name="psum", bufs=1))
        ctx.enter_context(tc.manual_schedule())

        def one_tile(x, i):
            return x.rearrange("(s p j) f -> s j p f", p=P, j=2)[i // 2, i % 2]

        def tile_couple(x, s):
            return x.rearrange("(s p j) f -> s p (j f)", p=P, j=2)[s]

        def load(name, src):
            t = keep.tile(list(src.shape), BF16, name=name, align_bytes=64)
            nc.sync.dma_start(out=t[:], in_=src)
            return t

        ident = keep.tile([P, P], F32, name="ident")
        make_identity(nc, ident[:])
        wb_scale_rows = keep.tile([P, ERR_PASSES * D], U8, name="wb_scale_rows", align_bytes=64)
        nc.vector.memset(wb_scale_rows[:].bitcast(I32), 0)

        first_halves, pred_teach, dlog_rows, emb_rows, wa_rows, wb_codes = {}, {}, {}, {}, {}, {}

        def load_first_half(h):
            cols = slice(h * HALF, (h + 1) * HALF)
            first_halves[h] = (load("pred0_%d" % h, one_tile(pred, 0)[:, cols]), load("teach0_%d" % h, one_tile(teach, 0)[:, cols]))

        def load_pred_teach(i):
            pred_teach[i] = (load("pred%d" % i, one_tile(pred, i))[:], load("teach%d" % i, one_tile(teach, i))[:])

        def load_dlog_couple(s):
            t = load("dlog_couple%d" % s, tile_couple(dlog, s))
            for j in range(2):
                dlog_rows[2 * s + j] = (t, j)

        def load_dlog_tile(i):
            dlog_rows[i] = (load("dlog%d" % i, one_tile(dlog, i)), 0)

        def load_emb(s):
            emb_rows[s] = load("emb%d" % s, tile_couple(emb, s))

        def load_wa(s):
            wa_rows[s] = load("wa%d" % s, tile_couple(wa, s))

        def load_wb(h):
            t = keep.tile([P, 2 * 2 * D], U8, name="wb%d" % h, align_bytes=64)
            nc.sync.dma_start(
                out=t[:].bitcast(I32).rearrange("p (g w) -> p g w", g=2),
                in_=wb_words[2 * h : 2 * h + 2].bitcast(I32).rearrange("g p w -> p g w"),
            )
            wb_codes[h] = t

        def load_wb_scales():
            rows = wb_scales.bitcast(I32).rearrange("g (q r) w -> r q g w", r=4)
            dst = wb_scale_rows[:].bitcast(I32).rearrange("p (g w) -> p g w", g=ERR_PASSES)
            for r in range(4):
                nc.sync.dma_start(out=dst[r:P:32], in_=rows[r])

        cw_cols = keep.tile([P, 4 * ERR_PASSES], BF16, name="cw_cols")

        def load_cw():
            nc.sync.dma_start(
                out=cw_cols[:].rearrange("p (g t) -> p g t", t=4),
                in_=cw.rearrange("(g p t) -> p g t", p=P, t=4),
            )

        load_first_half(0)
        load_cw()
        load_first_half(1)
        load_pred_teach(1)
        for s in range(D // (2 * P)):
            load_wa(s)
        load_dlog_couple(0)
        load_pred_teach(2)
        load_wb_scales()
        load_wb(0)
        load_wb(1)
        load_emb(0)
        load_dlog_tile(2)
        load_pred_teach(3)
        load_dlog_tile(3)
        for s in range(1, TILES // 2 - 1):
            load_pred_teach(2 * s + 2)
            load_emb(s)
            load_dlog_couple(s + 1)
            load_pred_teach(2 * s + 3)
        load_emb(TILES // 2 - 1)

        neg_cw = keep.tile([P, 4 * ERR_PASSES], BF16, name="neg_cw")
        nc.scalar.activation(out=neg_cw[:], in_=cw_cols[:], func=ACT.Copy, scale=-1.0)
        cw_bank = []
        for h in range(2):
            bank = psum.tile([P, BANK], F32, name="cw_bank%d" % h)
            for u in range(2):
                for g in range(2):
                    pair = 2 * (2 * h + g) + u
                    nc.tensor.transpose(
                        bank[:, (2 * u + g) * P : (2 * u + g + 1) * P],
                        neg_cw[:].bitcast(F32)[:, pair : pair + 1].to_broadcast([P, P]),
                        ident[:],
                    )
            cw_bank.append(bank)

        wa_grouped, wa_q, diff, err, err_grouped, err_q = {}, {}, {}, {}, {}, {}
        dlog_grouped, dlog_q, emb_sq, acc, result = {}, {}, {}, {}, {}

        def turn_bank(sources):
            bank = psum.tile([P, BANK], F32, name="turned", bufs=TURN_BANKS)
            for c, src in enumerate(sources):
                nc.tensor.transpose(bank[:, c * P : (c + 1) * P], src, ident[:])
            return bank

        def pairs_of_pass(rows, j, g, u):
            base = j * (C // 2) + g * (K_PASS // 2)
            return rows[:].bitcast(F32)[:, base + u : base + K_PASS // 2 : 2]

        def quantize(name, grouped, bufs, pool):
            width = grouped.shape[1] // 4
            codes = pool.tile([P, width], U32, name=name + "_codes", align_bytes=64, bufs=bufs)
            scales = pool.tile([P, width], U8, name=name + "_scales", align_bytes=64, bufs=bufs)
            nc.vector.quantize_mx(out=codes[:].bitcast(FP8X4), scales=scales[:], in_=grouped)
            return codes, scales

        def turn_wa(s):
            for g in range(LOG_PASSES):
                if s % 2 == 0:
                    wa_grouped[s // 2, g] = keep.tile(
                        [P, 4 * N_TILE], BF16, name="wa_grouped%d_%d" % (s // 2, g), align_bytes=64
                    )
                bank = turn_bank([pairs_of_pass(wa_rows[s], j, g, u) for j in range(2) for u in range(2)])
                dst = wa_grouped[s // 2, g][:].bitcast(F32)[:, (s % 2) * BANK : (s % 2 + 1) * BANK]
                nc.scalar.copy(
                    out=dst.rearrange("p (r ju) -> p r ju", ju=4), in_=bank[:].rearrange("p (ju r) -> p r ju", ju=4)
                )

        def quantize_wa(n):
            for g in range(LOG_PASSES):
                wa_q[n, g] = quantize("wa%d_%d" % (n, g), wa_grouped[n, g][:], 1, keep)

        def new_diff(i):
            diff[i] = work.tile([P, F], F32, name="diff%d" % i, tag="stage%d" % (i % 2), align_bytes=64)

        def subtract(engine, i, lo, hi):
            pred_i, teach_i = pred_teach[i]
            engine.tensor_tensor(out=diff[i][:, lo:hi], in0=pred_i[:, lo:hi], in1=teach_i[:, lo:hi], op=ALU.subtract)

        def subtract_first():
            new_diff(0)
            for h in range(2):
                pred_h, teach_h = first_halves[h]
                nc.vector.tensor_tensor(
                    out=diff[0][:, h * HALF : (h + 1) * HALF], in0=pred_h[:], in1=teach_h[:], op=ALU.subtract
                )

        def subtract_pool(i):
            new_diff(i)
            subtract(nc.gpsimd, i, 0, POOL_COLS)

        def subtract_vector(i):
            if i < POOL_FROM:
                new_diff(i)
                subtract(nc.vector, i, 0, F)
            else:
                subtract(nc.vector, i, POOL_COLS, F)

        def weigh(i):
            for h in range(2):
                t = work.tile([P, HALF], BF16, name="err", bufs=4, align_bytes=64)
                nc.vector.tensor_tensor(
                    out=t[:].rearrange("m (u q e) -> m u q e", u=2, e=2),
                    in0=diff[i][:, h * HALF : (h + 1) * HALF].rearrange("m (q u e) -> m u q e", u=2, e=2),
                    in1=cw_bank[h][:].bitcast(BF16).rearrange("m (u q e) -> m u q e", u=2, e=2),
                    op=ALU.mult,
                )
                err[i, h] = t

        def turn_err(i):
            err_grouped[i] = work.tile([P, F], BF16, name="err_grouped%d" % i, tag="stage%d" % (i % 2), align_bytes=64)
            for h in range(2):
                pairs = err[i, h][:].bitcast(F32)
                bank = turn_bank([pairs[:, (2 * u + g) * P : (2 * u + g + 1) * P] for g in range(2) for u in range(2)])
                dst = err_grouped[i][:].bitcast(F32)[:, h * BANK : (h + 1) * BANK]
                nc.scalar.copy(
                    out=dst.rearrange("p (g r u) -> p g r u", g=2, u=2),
                    in_=bank[:].rearrange("p (g u r) -> p g r u", g=2, u=2),
                )

        def turn_dlog(i):
            rows, j = dlog_rows[i]
            bank = turn_bank([pairs_of_pass(rows, j, g, u) for g in range(LOG_PASSES) for u in range(2)])
            t = work.tile([P, C], BF16, name="dlog_grouped", bufs=OPERAND_BUFS, align_bytes=64)
            for g in range(LOG_PASSES):
                cols = slice(g * K_PASS, (g + 1) * K_PASS)
                nc.scalar.activation(
                    out=t[:, cols].rearrange("p (r u e) -> p r u e", u=2, e=2),
                    in_=bank[:].bitcast(BF16)[:, cols].rearrange("p (u r e) -> p r u e", u=2, e=2),
                    func=ACT.Copy,
                    scale=-1.0,
                )
            dlog_grouped[i] = t

        def quantize_dlog(i):
            dlog_q[i] = quantize("dlog", dlog_grouped[i][:], OPERAND_BUFS, work)

        def quantize_err(i):
            codes, scales = quantize("err", err_grouped[i][:], OPERAND_BUFS, work)
            for g in range(ERR_PASSES):
                err_q[i, g] = (codes[:, g * P : (g + 1) * P], scales[:, g * P : (g + 1) * P])

        def quantize_err_half(i, h):
            codes, scales = quantize("err_half", err_grouped[i][:, h * HALF : (h + 1) * HALF], 2, work)
            for g in range(2):
                err_q[i, 2 * h + g] = (codes[:, g * P : (g + 1) * P], scales[:, g * P : (g + 1) * P])

        def square(i):
            t = work.tile([P, D], F32, name="emb_sq", bufs=OPERAND_BUFS)
            nc.scalar.activation(out=t[:], in_=emb_rows[i // 2][:, (i % 2) * D : (i % 2 + 1) * D], func=ACT.Square)
            emb_sq[i] = t

        def multiply_dlog(i, n):
            acc[i, n] = psum.tile([P, N_TILE], F32, name="acc", bufs=ACC_BANKS)
            codes, scales = dlog_q[i]
            for g in range(LOG_PASSES):
                nc.tensor.matmul_mx(
                    out=acc[i, n][:],
                    lhsT=codes[:, g * P : (g + 1) * P].bitcast(FP8X4),
                    lhsT_scale=scales[:, g * P : (g + 1) * P],
                    rhs=wa_q[n, g][0][:].bitcast(FP8X4),
                    rhs_scale=wa_q[n, g][1][:],
                    start=(g == 0),
                    stop=False,
                )

        def multiply_err(i, n, passes=range(ERR_PASSES)):
            for g in passes:
                byte0 = (g % 2) * 2 * D + n * 2 * N_TILE
                col0 = g * D + n * N_TILE
                nc.tensor.matmul_mx(
                    out=acc[i, n][:],
                    lhsT=err_q[i, g][0].bitcast(FP8X4),
                    lhsT_scale=err_q[i, g][1],
                    rhs=wb_codes[g // 2][:, byte0 : byte0 + 2 * N_TILE].bitcast(FP4X4),
                    rhs_scale=wb_scale_rows[:, col0 : col0 + N_TILE],
                    start=False,
                    stop=(g == ERR_PASSES - 1),
                )

        def finish(i, n):
            cols = slice(n * N_TILE, (n + 1) * N_TILE)
            if n == 0:
                result[i] = work.tile([P, D], F32, name="result", bufs=RESULT_BUFS)
            nc.vector.scalar_tensor_tensor(
                out=result[i][:, cols],
                in0=emb_sq[i][:, cols],
                scalar=1.0,
                in1=acc[i, n][:],
                op0=ALU.subtract,
                op1=ALU.mult,
            )
            if i == TILES - 1:
                nc.sync.dma_start(out=one_tile(out, i)[:, cols], in_=result[i][:, cols])
            elif n == 1:
                nc.sync.dma_start(out=one_tile(out, i), in_=result[i][:])

        subtract_first()
        weigh(0)
        turn_err(0)
        subtract_vector(1)
        quantize_err(0)
        weigh(1)
        for s in range(D // (2 * P)):
            turn_wa(s)
        quantize_wa(0)
        quantize_wa(1)
        turn_dlog(0)
        quantize_dlog(0)
        turn_err(1)
        turn_dlog(1)
        subtract_vector(2)
        quantize_dlog(1)
        quantize_err(1)

        multiply_dlog(0, 0)
        multiply_dlog(0, 1)
        multiply_err(0, 0)
        multiply_err(0, 1)
        square(0)
        weigh(2)
        finish(0, 0)
        finish(0, 1)
        multiply_dlog(1, 0)
        multiply_err(1, 0)
        square(1)
        finish(1, 0)
        turn_dlog(2)
        turn_err(2)
        multiply_dlog(1, 1)
        multiply_err(1, 1)
        subtract_vector(3)
        turn_dlog(3)
        square(2)
        quantize_dlog(2)
        quantize_err(2)

        last = TILES - 1
        for i in range(POOL_FROM - 1, last):
            subtract_pool(i + 1)
            weigh(i)
            finish(i - 2, 1)
            multiply_dlog(i - 1, 0)
            multiply_err(i - 1, 0)
            finish(i - 1, 0)
            multiply_dlog(i - 1, 1)
            turn_err(i)
            turn_dlog(i + 1)
            square(i)
            multiply_err(i - 1, 1)
            subtract_vector(i + 1)
            quantize_dlog(i)
            quantize_err(i)

        weigh(last)
        finish(last - 2, 1)
        multiply_dlog(last - 1, 0)
        multiply_err(last - 1, 0)
        multiply_dlog(last - 1, 1)
        multiply_err(last - 1, 1, range(2))
        turn_err(last)
        square(last)
        multiply_err(last - 1, 1, range(2, ERR_PASSES))
        quantize_dlog(last)
        finish(last - 1, 0)
        quantize_err_half(last, 0)
        quantize_err_half(last, 1)
        finish(last - 1, 1)
        multiply_dlog(last, 0)
        multiply_dlog(last, 1)
        multiply_err(last, 0)
        finish(last, 0)
        multiply_err(last, 1)
        finish(last, 1)
